import numpy as np
import ml_dtypes


def mxq(x, axis, fmt="e4m3"):
    dtype, down = {"e4m3": (ml_dtypes.float8_e4m3fn, 7), "e5m2": (ml_dtypes.float8_e5m2, 14)}[fmt]
    v = np.moveaxis(np.asarray(x, np.float32).astype(ml_dtypes.bfloat16).astype(np.float64), axis, -1)
    blocks = v.reshape(v.shape[:-1] + (-1, 32))
    amax = np.abs(blocks).max(-1, keepdims=True)
    byte = np.maximum(np.where(amax > 0, np.frexp(amax)[1] - 1 + 127, 0) - down, 1)
    scale = np.exp2(byte - 127.0)
    codes = (blocks / scale).astype(np.float32).astype(dtype).astype(np.float64)
    return np.moveaxis((codes * scale).reshape(v.shape), -1, axis)


WIDE = False


def mx_kscale(k):
    if not WIDE:
        return np.ones(k)
    levels = np.array([10, -10, 5, -5, 0])
    if k % 512:
        return np.exp2(np.random.permutation(np.resize(levels, k // 32))).repeat(32)
    a = np.empty((k // 512, 16))
    for p in range(k // 512):
        a[p, :8] = np.random.permutation(np.resize(levels, 8))
        for g in range(8):
            far = levels[np.abs(levels - a[p, g]) >= 10]
            a[p, g + 8] = far[np.random.randint(len(far))]
    return np.exp2(a.ravel()).repeat(32)


def f64(x):
    return np.asarray(x).astype(np.float64)


def striped(idx):
    return np.tile(idx.reshape(-1, 16).T, (8, 1)).astype(np.uint16)


def unstriped(offs):
    return offs[:16].T.reshape(-1).astype(np.int64)


def pack_weight(w):
    k, n = w.shape
    w = f64(np.asarray(w, np.float32).astype(ml_dtypes.bfloat16)).reshape(k // 32, 32, n)
    amax = np.abs(w).max(1)
    byte = np.clip(np.where(amax > 0, np.frexp(amax)[1] - 1 + 127 - 7, 1), 1, 254)
    scaled = (w * np.exp2(127.0 - byte)[:, None, :]).reshape(k, n).astype(np.float32)
    words = np.ascontiguousarray(scaled.reshape(k // 512, 128, 4, n).transpose(0, 1, 3, 2)).astype(ml_dtypes.float8_e4m3fn).view(np.uint8)
    return words, np.ascontiguousarray(byte.astype(np.uint8).reshape(k // 512, 16, n))


def unpack_weight(words, scales):
    g, p, n, _ = words.shape
    vals = np.ascontiguousarray(words).view(ml_dtypes.float8_e4m3fn).astype(np.float64) * np.repeat(np.exp2(scales.astype(np.float64) - 127.0), 8, axis=1)[..., None]
    return vals.transpose(0, 1, 3, 2).reshape(g * 512, n)


K, T, S, N = 512, 2048, 512, 256


def setup_inputs():
    n = np.random.standard_normal
    s = mx_kscale(K)[:, None]
    packed_xT = pack_weight(n((K, T)) * s)
    return {
        "x_words": packed_xT[0],
        "x_scales": packed_xT[1],
        "w1": (n((K, N)) / np.sqrt(K) / s).astype(np.float32),
        "w2": (n((K, N)) / np.sqrt(K) / s).astype(np.float32),
        "inten": (np.random.uniform(0.2, 2.0, (N, S))).astype(np.float32),
        "offs": striped(np.random.permutation(T)[:S]),
        "up": striped(np.random.permutation(S)),
        "upb": striped(np.random.permutation(S)),
    }


def reference(x_words, x_scales, w1, w2, inten, offs, up, upb):
    xq = unpack_weight(x_words, x_scales)[:, unstriped(offs)]
    yk = mxq(f64(w1), 0, "e4m3").T @ xq
    tau = np.log(np.exp(yk) + 1.0)
    tra = np.exp(-1.0 * tau)
    ys = mxq(f64(w2), 0, "e4m3").T @ xq
    src = np.exp(0.5 * ys)
    fac = (-1.0 * tra + 1.0) / (tau + 0.05)
    return f64(inten)[:, unstriped(up)] * tra + src * (-1.0 * fac + 1.0) + src[:, unstriped(upb)] * (fac - tra)

@@ -1,0 +1,145 @@
+from contextlib import ExitStack
+
+import concourse.mybir as mybir
+
+K, T, S, N = 512, 2048, 512, 256
+FLOPS = 2 * 2 * K * S * N
+
+F32 = mybir.dt.float32
+BF16 = mybir.dt.bfloat16
+I32 = mybir.dt.int32
+U32 = mybir.dt.uint32
+U16 = mybir.dt.uint16
+U8 = mybir.dt.uint8
+FP8X4 = mybir.dt.float8_e4m3fn_x4
+ACT = mybir.ActivationFunctionType
+ALU = mybir.AluOpType
+
+P = 128
+PACK = 4
+BLOCKS = N // P
+HALF = S // 2
+DEPTH_FLOOR = 0.05
+LN_GUARD = 2.0**-60
+
+
+def tile_picked_yrte_lin_p_kernel(tc, x_words, x_scales, w1, w2, inten, offs, up, upb, out):
+    nc = tc.nc
+    with ExitStack() as ctx:
+        keep = ctx.enter_context(tc.tile_pool(name="keep", bufs=1))
+        psum = ctx.enter_context(tc.psum_pool(name="psum", bufs=1))
+
+        offs_sb = keep.tile([P, S // 16], U16, name="offs_sb")
+        up_sb = keep.tile([P, S // 16], U16, name="up_sb")
+        upb_sb = keep.tile([P, S // 16], U16, name="upb_sb")
+        table_words = keep.tile([P, T], I32, name="table_words", align_bytes=64)
+        table_scales = keep.tile([P, T], U8, name="table_scales", tag="slot_b", align_bytes=64)
+        w2_raw = keep.tile([P, PACK, N], F32, name="w2_raw", tag="w_raw")
+
+        nc.vector.memset(table_scales[:].bitcast(I32), 0)
+        nc.sync.dma_start(offs_sb[:], offs)
+        nc.sync.dma_start(w2_raw[:], w2.rearrange("(p j) c -> p j c", j=PACK))
+        for q in range(4):
+            nc.scalar.dma_start(
+                table_scales[32 * q : 32 * q + 4, :].bitcast(I32),
+                x_scales[0, 4 * q : 4 * q + 4, :].bitcast(I32),
+            )
+        nc.sync.dma_start(table_words[:], x_words[0].rearrange("p n t -> p (n t)").bitcast(I32))
+        nc.sync.dma_start(upb_sb[:], upb)
+        nc.sync.dma_start(up_sb[:], up)
+
+        cell_words = keep.tile([P, S], U32, name="cell_words", align_bytes=64)
+        cell_scales = keep.tile([P, S], U8, name="cell_scales", align_bytes=64)
+
+        def interleave(raw, name, tag):
+            grouped = keep.tile([P, N, PACK], BF16, name=name, tag=tag, align_bytes=64)
+            nc.vector.tensor_copy(
+                grouped[:].rearrange("p (c i) j -> p c j i", i=4),
+                raw[:].rearrange("p j (c i) -> p c j i", i=4),
+            )
+            return grouped
+
+        def quantize(grouped, name):
+            codes = keep.tile([P, N], U32, name=name + "_codes", align_bytes=64)
+            scales = keep.tile([P, N], U8, name=name + "_scales", align_bytes=64)
+            nc.vector.quantize_mx(
+                out=codes[:].bitcast(FP8X4), scales=scales[:], in_=grouped[:].rearrange("p c j -> p (c j)")
+            )
+            return codes, scales
+
+        def product(codes, scales, b, cells, name):
+            acc = psum.tile([P, cells.stop - cells.start], F32, name=name)
+            cols = slice(b * P, (b + 1) * P)
+            nc.tensor.matmul_mx(
+                out=acc[:],
+                lhsT=codes[:, cols].bitcast(FP8X4),
+                lhsT_scale=scales[:, cols],
+                rhs=cell_words[:, cells].bitcast(FP8X4),
+                rhs_scale=cell_scales[:, cells],
+                start=True,
+                stop=True,
+            )
+            return acc
+
+        def planes(name):
+            return [keep.tile([P, S], F32, name="%s%d" % (name, b)) for b in range(BLOCKS)]
+
+        halves = [slice(h * HALF, (h + 1) * HALF) for h in range(2)]
+        entries = [slice(h * HALF // 16, (h + 1) * HALF // 16) for h in range(2)]
+        whole = slice(0, S)
+
+        w2_codes, w2_scales = quantize(interleave(w2_raw, "w2_grouped", "slot_a"), "w2")
+        w1_raw = keep.tile([P, PACK, N], F32, name="w1_raw", tag="w_raw")
+        nc.sync.dma_start(w1_raw[:], w1.rearrange("(p j) c -> p j c", j=PACK))
+        nc.vector.tensor_copy(cell_scales[:], table_scales[:].indirect(offs_sb[:]))
+        inten_sb = []
+        for b, tag in enumerate(("slot_a", "slot_b")):
+            rows = keep.tile([P, S], F32, name="inten%d" % b, tag=tag, align_bytes=64)
+            nc.sync.dma_start(rows[:], inten[b * P : (b + 1) * P, :])
+            inten_sb.append(rows)
+        for h in range(2):
+            nc.vector.tensor_copy(cell_words[:, halves[h]], table_words[:].bitcast(U32).indirect(offs_sb[:, entries[h]]))
+        ys0 = [product(w2_codes, w2_scales, 0, halves[h], "ys0_%d" % h) for h in range(2)]
+        ys1 = product(w2_codes, w2_scales, 1, whole, "ys1")
+        w1_codes, w1_scales = quantize(interleave(w1_raw, "w1_grouped", "w1_grouped"), "w1")
+        yk = [product(w1_codes, w1_scales, b, whole, "yk%d" % b) for b in range(BLOCKS)]
+
+        src, tra, ln_tra, tau = planes("src"), planes("tra"), planes("ln_tra"), planes("tau")
+        root, inv_depth = planes("root"), planes("inv_depth")
+        for h in range(2):
+            nc.scalar.activation(src[0][:, halves[h]], ys0[h][:], ACT.Exp, scale=0.5)
+        nc.scalar.activation(src[1][:], ys1[:], ACT.Exp, scale=0.5)
+        for b in range(BLOCKS):
+            nc.scalar.activation(tra[b][:], yk[b][:], ACT.Sigmoid, scale=-1.0)
+        for b in range(BLOCKS):
+            nc.scalar.activation(ln_tra[b][:], tra[b][:], ACT.Ln, bias=LN_GUARD)
+        for b in range(BLOCKS):
+            nc.vector.scalar_tensor_tensor(tau[b][:], ln_tra[b][:], -1.0, yk[b][:], ALU.mult, ALU.max)
+        for b in range(BLOCKS):
+            nc.scalar.activation(root[b][:], tau[b][:], ACT.Abs_reciprocal_sqrt, bias=DEPTH_FLOOR)
+            nc.scalar.activation(inv_depth[b][:], root[b][:], ACT.Square)
+
+        src_b, diff, step, through, base = planes("src_b"), planes("diff"), planes("step"), planes("through"), planes("base")
+        shared, result = planes("shared"), planes("result")
+        for b in range(BLOCKS):
+            for h in range(2):
+                nc.vector.tensor_copy(src_b[b][:, halves[h]], src[b][:].indirect(upb_sb[:, entries[h]]))
+            for h in range(2):
+                nc.vector.tensor_tensor(
+                    diff[b][:, halves[h]], inten_sb[b][:].indirect(up_sb[:, entries[h]]), src_b[b][:, halves[h]], ALU.subtract
+                )
+            nc.vector.tensor_tensor(step[b][:], src_b[b][:], src[b][:], ALU.subtract)
+        nc.vector.tensor_tensor(through[0][:], diff[0][:], tra[0][:], ALU.mult)
+        nc.vector.tensor_tensor(base[0][:], through[0][:], src[0][:], ALU.add)
+        emitted0, through1 = ln_tra[0], ln_tra[1]
+        nc.vector.scalar_tensor_tensor(emitted0[:], tra[0][:], 1.0, step[0][:], ALU.subtract, ALU.mult)
+        nc.vector.tensor_tensor(through1[:], diff[1][:], tra[1][:], ALU.mult)
+        nc.vector.tensor_tensor(shared[0][:], emitted0[:], inv_depth[0][:], ALU.mult)
+        nc.vector.tensor_tensor(result[0][:], base[0][:], shared[0][:], ALU.subtract)
+        nc.sync.dma_start(out[0:P, :], result[0][:])
+        emitted1 = through[1]
+        nc.vector.tensor_tensor(base[1][:], through1[:], src[1][:], ALU.add)
+        nc.vector.scalar_tensor_tensor(emitted1[:], tra[1][:], 1.0, step[1][:], ALU.subtract, ALU.mult)
+        nc.vector.tensor_tensor(shared[1][:], emitted1[:], inv_depth[1][:], ALU.mult)
+        nc.vector.tensor_tensor(result[1][:], base[1][:], shared[1][:], ALU.subtract)
+        nc.sync.dma_start(out[P : 2 * P, :], result[1][:])

@@ -33,27 +33,32 @@ def tile_picked_yrte_lin_p_kernel(tc, x_words, x_scales, w1, w2, inten, offs, up
         up_sb = keep.tile([P, S // 16], U16, name="up_sb")
         upb_sb = keep.tile([P, S // 16], U16, name="upb_sb")
         table_words = keep.tile([P, T], I32, name="table_words", align_bytes=64)
-        table_scales = keep.tile([P, T], U8, name="table_scales", tag="slot_b", align_bytes=64)
-        w2_raw = keep.tile([P, PACK, N], F32, name="w2_raw", tag="w_raw")
+        table_scales = keep.tile([P, T], U8, name="table_scales", align_bytes=64)
+        w1_raw = keep.tile([P, PACK, N], F32, name="w1_raw", tag="staging")
+        w2_raw = keep.tile([P, PACK, N], F32, name="w2_raw")
+        inten_sb = [keep.tile([P, S], F32, name="inten%d" % b) for b in range(BLOCKS)]
 
         nc.vector.memset(table_scales[:].bitcast(I32), 0)
         nc.sync.dma_start(offs_sb[:], offs)
         nc.sync.dma_start(w2_raw[:], w2.rearrange("(p j) c -> p j c", j=PACK))
         for q in range(4):
-            nc.scalar.dma_start(
+            nc.sync.dma_start(
                 table_scales[32 * q : 32 * q + 4, :].bitcast(I32),
                 x_scales[0, 4 * q : 4 * q + 4, :].bitcast(I32),
             )
         nc.sync.dma_start(table_words[:], x_words[0].rearrange("p n t -> p (n t)").bitcast(I32))
+        nc.sync.dma_start(w1_raw[:], w1.rearrange("(p j) c -> p j c", j=PACK))
         nc.sync.dma_start(upb_sb[:], upb)
         nc.sync.dma_start(up_sb[:], up)
+        for b in range(BLOCKS):
+            nc.sync.dma_start(inten_sb[b][:], inten[b * P : (b + 1) * P, :])
 
         cell_words = keep.tile([P, S], U32, name="cell_words", align_bytes=64)
         cell_scales = keep.tile([P, S], U8, name="cell_scales", align_bytes=64)
 
-        def interleave(raw, name, tag):
-            grouped = keep.tile([P, N, PACK], BF16, name=name, tag=tag, align_bytes=64)
-            nc.vector.tensor_copy(
+        def interleave(copy, raw, name):
+            grouped = keep.tile([P, N, PACK], BF16, name=name, align_bytes=64)
+            copy(
                 grouped[:].rearrange("p (c i) j -> p c j i", i=4),
                 raw[:].rearrange("p j (c i) -> p c j i", i=4),
             )
@@ -88,20 +93,13 @@ def tile_picked_yrte_lin_p_kernel(tc, x_words, x_scales, w1, w2, inten, offs, up
         entries = [slice(h * HALF // 16, (h + 1) * HALF // 16) for h in range(2)]
         whole = slice(0, S)
 
-        w2_codes, w2_scales = quantize(interleave(w2_raw, "w2_grouped", "slot_a"), "w2")
-        w1_raw = keep.tile([P, PACK, N], F32, name="w1_raw", tag="w_raw")
-        nc.sync.dma_start(w1_raw[:], w1.rearrange("(p j) c -> p j c", j=PACK))
         nc.vector.tensor_copy(cell_scales[:], table_scales[:].indirect(offs_sb[:]))
-        inten_sb = []
-        for b, tag in enumerate(("slot_a", "slot_b")):
-            rows = keep.tile([P, S], F32, name="inten%d" % b, tag=tag, align_bytes=64)
-            nc.sync.dma_start(rows[:], inten[b * P : (b + 1) * P, :])
-            inten_sb.append(rows)
+        w2_codes, w2_scales = quantize(interleave(nc.scalar.copy, w2_raw, "w2_grouped"), "w2")
         for h in range(2):
             nc.vector.tensor_copy(cell_words[:, halves[h]], table_words[:].bitcast(U32).indirect(offs_sb[:, entries[h]]))
         ys0 = [product(w2_codes, w2_scales, 0, halves[h], "ys0_%d" % h) for h in range(2)]
         ys1 = product(w2_codes, w2_scales, 1, whole, "ys1")
-        w1_codes, w1_scales = quantize(interleave(w1_raw, "w1_grouped", "w1_grouped"), "w1")
+        w1_codes, w1_scales = quantize(interleave(nc.vector.tensor_copy, w1_raw, "w1_grouped"), "w1")
         yk = [product(w1_codes, w1_scales, b, whole, "yk%d" % b) for b in range(BLOCKS)]
 
         src, tra, ln_tra, tau = planes("src"), planes("tra"), planes("ln_tra"), planes("tau")
@@ -119,7 +117,9 @@ def tile_picked_yrte_lin_p_kernel(tc, x_words, x_scales, w1, w2, inten, offs, up
             nc.scalar.activation(root[b][:], tau[b][:], ACT.Abs_reciprocal_sqrt, bias=DEPTH_FLOOR)
             nc.scalar.activation(inv_depth[b][:], root[b][:], ACT.Square)
 
-        src_b, diff, step, through, base = planes("src_b"), planes("diff"), planes("step"), planes("through"), planes("base")
+        fetched = keep.tile([P, BLOCKS, S], F32, name="fetched", tag="staging")
+        src_b = [fetched[:, b, :] for b in range(BLOCKS)]
+        diff, step, through = planes("diff"), planes("step"), planes("through")
         shared, result = planes("shared"), planes("result")
         for b in range(BLOCKS):
             for h in range(2):
@@ -128,18 +128,21 @@ def tile_picked_yrte_lin_p_kernel(tc, x_words, x_scales, w1, w2, inten, offs, up
                 nc.vector.tensor_tensor(
                     diff[b][:, halves[h]], inten_sb[b][:].indirect(up_sb[:, entries[h]]), src_b[b][:, halves[h]], ALU.subtract
                 )
-            nc.vector.tensor_tensor(step[b][:], src_b[b][:], src[b][:], ALU.subtract)
+            nc.vector.tensor_tensor(step[b][:], src_b[b], src[b][:], ALU.subtract)
+        emitted = planes("emitted")
         nc.vector.tensor_tensor(through[0][:], diff[0][:], tra[0][:], ALU.mult)
-        nc.vector.tensor_tensor(base[0][:], through[0][:], src[0][:], ALU.add)
-        emitted0, through1 = ln_tra[0], ln_tra[1]
-        nc.vector.scalar_tensor_tensor(emitted0[:], tra[0][:], 1.0, step[0][:], ALU.subtract, ALU.mult)
-        nc.vector.tensor_tensor(through1[:], diff[1][:], tra[1][:], ALU.mult)
-        nc.vector.tensor_tensor(shared[0][:], emitted0[:], inv_depth[0][:], ALU.mult)
-        nc.vector.tensor_tensor(result[0][:], base[0][:], shared[0][:], ALU.subtract)
-        nc.sync.dma_start(out[0:P, :], result[0][:])
-        emitted1 = through[1]
-        nc.vector.tensor_tensor(base[1][:], through1[:], src[1][:], ALU.add)
+        nc.vector.scalar_tensor_tensor(emitted[0][:], tra[0][:], 1.0, step[0][:], ALU.subtract, ALU.mult)
+        nc.vector.tensor_tensor(through[1][:], diff[1][:], tra[1][:], ALU.mult)
+        base0, emitted1 = ln_tra[0], ln_tra[1]
+        nc.vector.tensor_tensor(base0[:], through[0][:], src[0][:], ALU.add)
         nc.vector.scalar_tensor_tensor(emitted1[:], tra[1][:], 1.0, step[1][:], ALU.subtract, ALU.mult)
-        nc.vector.tensor_tensor(shared[1][:], emitted1[:], inv_depth[1][:], ALU.mult)
-        nc.vector.tensor_tensor(result[1][:], base[1][:], shared[1][:], ALU.subtract)
-        nc.sync.dma_start(out[P : 2 * P, :], result[1][:])
+        base1 = through[0]
+        nc.vector.tensor_tensor(base1[:], through[1][:], src[1][:], ALU.add)
+        for b, (bs, em) in enumerate(((base0, emitted[0]), (base1, emitted1))):
+            for h in range(2):
+                nc.vector.tensor_tensor(shared[b][:, halves[h]], em[:, halves[h]], inv_depth[b][:, halves[h]], ALU.mult)
+            for h in range(2):
+                nc.vector.tensor_tensor(result[b][:, halves[h]], bs[:, halves[h]], shared[b][:, halves[h]], ALU.subtract)
+        nc.sync.dma_start(out[0:P, :], result[0][:])
+        nc.sync.dma_start(out[P : 2 * P, halves[0]], result[1][:, halves[0]])
+        nc.scalar.dma_start(out[P : 2 * P, halves[1]], result[1][:, halves[1]])

@@ -102,24 +102,28 @@ def tile_picked_yrte_lin_p_kernel(tc, x_words, x_scales, w1, w2, inten, offs, up
         w1_codes, w1_scales = quantize(interleave(nc.vector.tensor_copy, w1_raw, "w1_grouped"), "w1")
         yk = [product(w1_codes, w1_scales, b, whole, "yk%d" % b) for b in range(BLOCKS)]
 
-        src, tra, ln_tra, tau = planes("src"), planes("tra"), planes("ln_tra"), planes("tau")
+        src, tau = planes("src"), planes("tau")
+        tra_all = keep.tile([P, BLOCKS, S], F32, name="tra_all")
+        ln_all = keep.tile([P, BLOCKS, S], F32, name="ln_all")
+        tra = [tra_all[:, b, :] for b in range(BLOCKS)]
+        ln_tra = [ln_all[:, b, :] for b in range(BLOCKS)]
         root, inv_depth = planes("root"), planes("inv_depth")
         for h in range(2):
             nc.scalar.activation(src[0][:, halves[h]], ys0[h][:], ACT.Exp, scale=0.5)
         nc.scalar.activation(src[1][:], ys1[:], ACT.Exp, scale=0.5)
         for b in range(BLOCKS):
-            nc.scalar.activation(tra[b][:], yk[b][:], ACT.Sigmoid, scale=-1.0)
+            nc.scalar.activation(tra[b], yk[b][:], ACT.Sigmoid, scale=-1.0)
+        nc.scalar.activation(ln_all[:], tra_all[:], ACT.Ln, bias=LN_GUARD)
         for b in range(BLOCKS):
-            nc.scalar.activation(ln_tra[b][:], tra[b][:], ACT.Ln, bias=LN_GUARD)
-        for b in range(BLOCKS):
-            nc.vector.scalar_tensor_tensor(tau[b][:], ln_tra[b][:], -1.0, yk[b][:], ALU.mult, ALU.max)
+            nc.vector.scalar_tensor_tensor(tau[b][:], ln_tra[b], -1.0, yk[b][:], ALU.mult, ALU.max)
         for b in range(BLOCKS):
             nc.scalar.activation(root[b][:], tau[b][:], ACT.Abs_reciprocal_sqrt, bias=DEPTH_FLOOR)
             nc.scalar.activation(inv_depth[b][:], root[b][:], ACT.Square)
 
         fetched = keep.tile([P, BLOCKS, S], F32, name="fetched", tag="staging")
         src_b = [fetched[:, b, :] for b in range(BLOCKS)]
-        diff, step, through = planes("diff"), planes("step"), planes("through")
+        diff = planes("diff")
+        step = []
         shared, result = planes("shared"), planes("result")
         for b in range(BLOCKS):
             for h in range(2):
@@ -128,17 +132,20 @@ def tile_picked_yrte_lin_p_kernel(tc, x_words, x_scales, w1, w2, inten, offs, up
                 nc.vector.tensor_tensor(
                     diff[b][:, halves[h]], inten_sb[b][:].indirect(up_sb[:, entries[h]]), src_b[b][:, halves[h]], ALU.subtract
                 )
-            nc.vector.tensor_tensor(step[b][:], src_b[b], src[b][:], ALU.subtract)
-        emitted = planes("emitted")
-        nc.vector.tensor_tensor(through[0][:], diff[0][:], tra[0][:], ALU.mult)
-        nc.vector.scalar_tensor_tensor(emitted[0][:], tra[0][:], 1.0, step[0][:], ALU.subtract, ALU.mult)
-        nc.vector.tensor_tensor(through[1][:], diff[1][:], tra[1][:], ALU.mult)
-        base0, emitted1 = ln_tra[0], ln_tra[1]
-        nc.vector.tensor_tensor(base0[:], through[0][:], src[0][:], ALU.add)
-        nc.vector.scalar_tensor_tensor(emitted1[:], tra[1][:], 1.0, step[1][:], ALU.subtract, ALU.mult)
-        base1 = through[0]
-        nc.vector.tensor_tensor(base1[:], through[1][:], src[1][:], ALU.add)
-        for b, (bs, em) in enumerate(((base0, emitted[0]), (base1, emitted1))):
+            step.append(keep.tile([P, S], F32, name="step%d" % b))
+            engine = nc.gpsimd if b == 0 else nc.vector
+            engine.tensor_tensor(step[b][:], src_b[b], src[b][:], ALU.subtract)
+        base0 = keep.tile([P, S], F32, name="base0")
+        base1 = keep.tile([P, S], F32, name="base1")
+        through0 = keep.tile([P, S], F32, name="through0")
+        nc.vector.tensor_tensor(through0[:], diff[0][:], tra[0], ALU.mult)
+        nc.gpsimd.tensor_tensor(base0[:], through0[:], src[0][:], ALU.add)
+        emitted0, through1, emitted1 = ln_tra[0], ln_tra[1], step[0]
+        nc.vector.scalar_tensor_tensor(emitted0, tra[0], 1.0, step[0][:], ALU.subtract, ALU.mult)
+        nc.vector.tensor_tensor(through1, diff[1][:], tra[1], ALU.mult)
+        nc.vector.scalar_tensor_tensor(emitted1[:], tra[1], 1.0, step[1][:], ALU.subtract, ALU.mult)
+        nc.vector.tensor_tensor(base1[:], through1, src[1][:], ALU.add)
+        for b, (bs, em) in enumerate(((base0, emitted0), (base1, emitted1))):
             for h in range(2):
                 nc.vector.tensor_tensor(shared[b][:, halves[h]], em[:, halves[h]], inv_depth[b][:, halves[h]], ALU.mult)
             for h in range(2):

@@ -97,8 +97,7 @@ def tile_picked_yrte_lin_p_kernel(tc, x_words, x_scales, w1, w2, inten, offs, up
         w2_codes, w2_scales = quantize(interleave(nc.scalar.copy, w2_raw, "w2_grouped"), "w2")
         for h in range(2):
             nc.vector.tensor_copy(cell_words[:, halves[h]], table_words[:].bitcast(U32).indirect(offs_sb[:, entries[h]]))
-        ys0 = [product(w2_codes, w2_scales, 0, halves[h], "ys0_%d" % h) for h in range(2)]
-        ys1 = product(w2_codes, w2_scales, 1, whole, "ys1")
+        ys = [[product(w2_codes, w2_scales, b, halves[h], "ys%d_%d" % (b, h)) for b in range(BLOCKS)] for h in range(2)]
         w1_codes, w1_scales = quantize(interleave(nc.vector.tensor_copy, w1_raw, "w1_grouped"), "w1")
         yk = [product(w1_codes, w1_scales, b, whole, "yk%d" % b) for b in range(BLOCKS)]
 
@@ -109,16 +108,18 @@ def tile_picked_yrte_lin_p_kernel(tc, x_words, x_scales, w1, w2, inten, offs, up
         ln_tra = [ln_all[:, b, :] for b in range(BLOCKS)]
         root, inv_depth = planes("root"), planes("inv_depth")
         for h in range(2):
-            nc.scalar.activation(src[0][:, halves[h]], ys0[h][:], ACT.Exp, scale=0.5)
-        nc.scalar.activation(src[1][:], ys1[:], ACT.Exp, scale=0.5)
+            for b in range(BLOCKS):
+                nc.scalar.activation(src[b][:, halves[h]], ys[h][b][:], ACT.Exp, scale=0.5)
         for b in range(BLOCKS):
             nc.scalar.activation(tra[b], yk[b][:], ACT.Sigmoid, scale=-1.0)
         nc.scalar.activation(ln_all[:], tra_all[:], ACT.Ln, bias=LN_GUARD)
         for b in range(BLOCKS):
             nc.vector.scalar_tensor_tensor(tau[b][:], ln_tra[b], -1.0, yk[b][:], ALU.mult, ALU.max)
         for b in range(BLOCKS):
-            nc.scalar.activation(root[b][:], tau[b][:], ACT.Abs_reciprocal_sqrt, bias=DEPTH_FLOOR)
-            nc.scalar.activation(inv_depth[b][:], root[b][:], ACT.Square)
+            for h in range(2):
+                nc.scalar.activation(root[b][:, halves[h]], tau[b][:, halves[h]], ACT.Abs_reciprocal_sqrt, bias=DEPTH_FLOOR)
+            for h in range(2):
+                nc.scalar.activation(inv_depth[b][:, halves[h]], root[b][:, halves[h]], ACT.Square)
 
         fetched = keep.tile([P, BLOCKS, S], F32, name="fetched", tag="staging")
         src_b = [fetched[:, b, :] for b in range(BLOCKS)]
@@ -133,8 +134,7 @@ def tile_picked_yrte_lin_p_kernel(tc, x_words, x_scales, w1, w2, inten, offs, up
                     diff[b][:, halves[h]], inten_sb[b][:].indirect(up_sb[:, entries[h]]), src_b[b][:, halves[h]], ALU.subtract
                 )
             step.append(keep.tile([P, S], F32, name="step%d" % b))
-            engine = nc.gpsimd if b == 0 else nc.vector
-            engine.tensor_tensor(step[b][:], src_b[b], src[b][:], ALU.subtract)
+            nc.vector.tensor_tensor(step[b][:], src_b[b], src[b][:], ALU.subtract)
         base0 = keep.tile([P, S], F32, name="base0")
         base1 = keep.tile([P, S], F32, name="base1")
         through0 = keep.tile([P, S], F32, name="through0")

from contextlib import ExitStack

import concourse.mybir as mybir

K, T, S, N = 512, 2048, 512, 256
FLOPS = 2 * 2 * K * S * N

F32 = mybir.dt.float32
BF16 = mybir.dt.bfloat16
I32 = mybir.dt.int32
U32 = mybir.dt.uint32
U16 = mybir.dt.uint16
U8 = mybir.dt.uint8
FP8X4 = mybir.dt.float8_e4m3fn_x4
ACT = mybir.ActivationFunctionType
ALU = mybir.AluOpType

P = 128
PACK = 4
BLOCKS = N // P
HALF = S // 2
DEPTH_FLOOR = 0.05
LN_GUARD = 2.0**-60


def tile_picked_yrte_lin_p_kernel(tc, x_words, x_scales, w1, w2, inten, offs, up, upb, out):
    nc = tc.nc
    with ExitStack() as ctx:
        keep = ctx.enter_context(tc.tile_pool(name="keep", bufs=1))
        psum = ctx.enter_context(tc.psum_pool(name="psum", bufs=1))

        offs_sb = keep.tile([P, S // 16], U16, name="offs_sb")
        up_sb = keep.tile([P, S // 16], U16, name="up_sb")
        upb_sb = keep.tile([P, S // 16], U16, name="upb_sb")
        table_words = keep.tile([P, T], I32, name="table_words", align_bytes=64)
        table_scales = keep.tile([P, T], U8, name="table_scales", align_bytes=64)
        w1_raw = keep.tile([P, PACK, N], F32, name="w1_raw", tag="staging")
        w2_raw = keep.tile([P, PACK, N], F32, name="w2_raw")
        inten_sb = [keep.tile([P, S], F32, name="inten%d" % b) for b in range(BLOCKS)]

        nc.vector.memset(table_scales[:].bitcast(I32), 0)
        nc.sync.dma_start(offs_sb[:], offs)
        nc.sync.dma_start(w2_raw[:], w2.rearrange("(p j) c -> p j c", j=PACK))
        for q in range(4):
            nc.sync.dma_start(
                table_scales[32 * q : 32 * q + 4, :].bitcast(I32),
                x_scales[0, 4 * q : 4 * q + 4, :].bitcast(I32),
            )
        nc.sync.dma_start(table_words[:], x_words[0].rearrange("p n t -> p (n t)").bitcast(I32))
        nc.sync.dma_start(w1_raw[:], w1.rearrange("(p j) c -> p j c", j=PACK))
        nc.sync.dma_start(upb_sb[:], upb)
        nc.sync.dma_start(up_sb[:], up)
        for b in range(BLOCKS):
            nc.sync.dma_start(inten_sb[b][:], inten[b * P : (b + 1) * P, :])

        cell_words = keep.tile([P, S], U32, name="cell_words", align_bytes=64)
        cell_scales = keep.tile([P, S], U8, name="cell_scales", align_bytes=64)

        def interleave(copy, raw, name):
            grouped = keep.tile([P, N, PACK], BF16, name=name, align_bytes=64)
            copy(
                grouped[:].rearrange("p (c i) j -> p c j i", i=4),
                raw[:].rearrange("p j (c i) -> p c j i", i=4),
            )
            return grouped

        def quantize(grouped, name):
            codes = keep.tile([P, N], U32, name=name + "_codes", align_bytes=64)
            scales = keep.tile([P, N], U8, name=name + "_scales", align_bytes=64)
            nc.vector.quantize_mx(
                out=codes[:].bitcast(FP8X4), scales=scales[:], in_=grouped[:].rearrange("p c j -> p (c j)")
            )
            return codes, scales

        def product(codes, scales, b, cells, name):
            acc = psum.tile([P, cells.stop - cells.start], F32, name=name)
            cols = slice(b * P, (b + 1) * P)
            nc.tensor.matmul_mx(
                out=acc[:],
                lhsT=codes[:, cols].bitcast(FP8X4),
                lhsT_scale=scales[:, cols],
                rhs=cell_words[:, cells].bitcast(FP8X4),
                rhs_scale=cell_scales[:, cells],
                start=True,
                stop=True,
            )
            return acc

        def planes(name):
            return [keep.tile([P, S], F32, name="%s%d" % (name, b)) for b in range(BLOCKS)]

        halves = [slice(h * HALF, (h + 1) * HALF) for h in range(2)]
        entries = [slice(h * HALF // 16, (h + 1) * HALF // 16) for h in range(2)]
        whole = slice(0, S)

        nc.vector.tensor_copy(cell_scales[:], table_scales[:].indirect(offs_sb[:]))
        w2_codes, w2_scales = quantize(interleave(nc.scalar.copy, w2_raw, "w2_grouped"), "w2")
        for h in range(2):
            nc.vector.tensor_copy(cell_words[:, halves[h]], table_words[:].bitcast(U32).indirect(offs_sb[:, entries[h]]))
        ys = [[product(w2_codes, w2_scales, b, halves[h], "ys%d_%d" % (b, h)) for b in range(BLOCKS)] for h in range(2)]
        w1_codes, w1_scales = quantize(interleave(nc.vector.tensor_copy, w1_raw, "w1_grouped"), "w1")
        yk = [product(w1_codes, w1_scales, b, whole, "yk%d" % b) for b in range(BLOCKS)]

        src, tau = planes("src"), planes("tau")
        tra_all = keep.tile([P, BLOCKS, S], F32, name="tra_all")
        ln_all = keep.tile([P, BLOCKS, S], F32, name="ln_all")
        tra = [tra_all[:, b, :] for b in range(BLOCKS)]
        ln_tra = [ln_all[:, b, :] for b in range(BLOCKS)]
        root, inv_depth = planes("root"), planes("inv_depth")
        for h in range(2):
            for b in range(BLOCKS):
                nc.scalar.activation(src[b][:, halves[h]], ys[h][b][:], ACT.Exp, scale=0.5)
        for b in range(BLOCKS):
            nc.scalar.activation(tra[b], yk[b][:], ACT.Sigmoid, scale=-1.0)
        nc.scalar.activation(ln_all[:], tra_all[:], ACT.Ln, bias=LN_GUARD)
        for b in range(BLOCKS):
            nc.vector.scalar_tensor_tensor(tau[b][:], ln_tra[b], -1.0, yk[b][:], ALU.mult, ALU.max)
        for b in range(BLOCKS):
            for h in range(2):
                nc.scalar.activation(root[b][:, halves[h]], tau[b][:, halves[h]], ACT.Abs_reciprocal_sqrt, bias=DEPTH_FLOOR)
            for h in range(2):
                nc.scalar.activation(inv_depth[b][:, halves[h]], root[b][:, halves[h]], ACT.Square)

        fetched = keep.tile([P, BLOCKS, S], F32, name="fetched", tag="staging")
        src_b = [fetched[:, b, :] for b in range(BLOCKS)]
        diff = planes("diff")
        step = []
        shared, result = planes("shared"), planes("result")
        for b in range(BLOCKS):
            for h in range(2):
                nc.vector.tensor_copy(src_b[b][:, halves[h]], src[b][:].indirect(upb_sb[:, entries[h]]))
            for h in range(2):
                nc.vector.tensor_tensor(
                    diff[b][:, halves[h]], inten_sb[b][:].indirect(up_sb[:, entries[h]]), src_b[b][:, halves[h]], ALU.subtract
                )
            step.append(keep.tile([P, S], F32, name="step%d" % b))
            nc.vector.tensor_tensor(step[b][:], src_b[b], src[b][:], ALU.subtract)
        base0 = keep.tile([P, S], F32, name="base0")
        base1 = keep.tile([P, S], F32, name="base1")
        through0 = keep.tile([P, S], F32, name="through0")
        nc.vector.tensor_tensor(through0[:], diff[0][:], tra[0], ALU.mult)
        nc.gpsimd.tensor_tensor(base0[:], through0[:], src[0][:], ALU.add)
        emitted0, through1, emitted1 = ln_tra[0], ln_tra[1], step[0]
        nc.vector.scalar_tensor_tensor(emitted0, tra[0], 1.0, step[0][:], ALU.subtract, ALU.mult)
        nc.vector.tensor_tensor(through1, diff[1][:], tra[1], ALU.mult)
        nc.vector.scalar_tensor_tensor(emitted1[:], tra[1], 1.0, step[1][:], ALU.subtract, ALU.mult)
        nc.vector.tensor_tensor(base1[:], through1, src[1][:], ALU.add)
        for b, (bs, em) in enumerate(((base0, emitted0), (base1, emitted1))):
            for h in range(2):
                nc.vector.tensor_tensor(shared[b][:, halves[h]], em[:, halves[h]], inv_depth[b][:, halves[h]], ALU.mult)
            for h in range(2):
                nc.vector.tensor_tensor(result[b][:, halves[h]], bs[:, halves[h]], shared[b][:, halves[h]], ALU.subtract)
        nc.sync.dma_start(out[0:P, :], result[0][:])
        nc.sync.dma_start(out[P : 2 * P, halves[0]], result[1][:, halves[0]])
        nc.scalar.dma_start(out[P : 2 * P, halves[1]], result[1][:, halves[1]])
